import numpy as np
import ml_dtypes


def mxq(x, axis, fmt="e4m3"):
    dtype, down = {"e4m3": (ml_dtypes.float8_e4m3fn, 7), "e5m2": (ml_dtypes.float8_e5m2, 14)}[fmt]
    v = np.moveaxis(np.asarray(x, np.float32).astype(ml_dtypes.bfloat16).astype(np.float64), axis, -1)
    blocks = v.reshape(v.shape[:-1] + (-1, 32))
    amax = np.abs(blocks).max(-1, keepdims=True)
    byte = np.maximum(np.where(amax > 0, np.frexp(amax)[1] - 1 + 127, 0) - down, 1)
    scale = np.exp2(byte - 127.0)
    codes = (blocks / scale).astype(np.float32).astype(dtype).astype(np.float64)
    return np.moveaxis((codes * scale).reshape(v.shape), -1, axis)


WIDE = False


def mx_kscale(k):
    if not WIDE:
        return np.ones(k)
    levels = np.array([10, -10, 5, -5, 0])
    if k % 512:
        return np.exp2(np.random.permutation(np.resize(levels, k // 32))).repeat(32)
    a = np.empty((k // 512, 16))
    for p in range(k // 512):
        a[p, :8] = np.random.permutation(np.resize(levels, 8))
        for g in range(8):
            far = levels[np.abs(levels - a[p, g]) >= 10]
            a[p, g + 8] = far[np.random.randint(len(far))]
    return np.exp2(a.ravel()).repeat(32)


def f64(x):
    return np.asarray(x).astype(np.float64)


def striped(idx):
    return np.tile(idx.reshape(-1, 16).T, (8, 1)).astype(np.uint16)


def unstriped(offs):
    return offs[:16].T.reshape(-1).astype(np.int64)


def gelu(v):
    return 0.5 * v * (1.0 + np.tanh(np.sqrt(2.0 / np.pi) * (v + 0.044715 * v**3)))


K, T, E, C, N = 1024, 512, 4, 128, 128


def by_expert(wq, xq):
    return np.concatenate([wq[e].T @ xq[:, e * C:(e + 1) * C] for e in range(E)], axis=1)


def setup_inputs():
    n = np.random.standard_normal
    s = mx_kscale(K)[:, None]
    return {
        "xT": (n((K, T)) * s).astype(np.float32),
        "w": (n((E, K, N)) / np.sqrt(K) / s[None]).astype(np.float32),
        "b": (0.3 * n((N, E))).astype(np.float32),
        "gate": np.tile(np.random.uniform(0.2, 1.0, E * C), (N, 1)).astype(np.float32),
        "offs": striped(np.random.permutation(T)[:E * C]),
    }


def reference(xT, w, b, gate, offs):
    idx = unstriped(offs)
    xq = mxq(f64(xT)[:, idx], 0, "e4m3")
    y = by_expert(mxq(f64(w), 1, "e4m3"), xq)
    y = gelu(y + np.repeat(f64(b), C, axis=1))
    out = np.zeros((N, T))
    out[:, idx] = f64(gate) * y
    return out

@@ -1,0 +1,148 @@
+from contextlib import ExitStack
+
+import concourse.mybir as mybir
+
+K, T, E, C, N = 1024, 512, 4, 128, 128
+S = E * C
+FLOPS = 2 * K * N * S
+
+F32 = mybir.dt.float32
+BF16 = mybir.dt.bfloat16
+U32 = mybir.dt.uint32
+U16 = mybir.dt.uint16
+U8 = mybir.dt.uint8
+FP8X4 = mybir.dt.float8_e4m3fn_x4
+GELU = mybir.ActivationFunctionType.Gelu_apprx_tanh
+MULT = mybir.AluOpType.mult
+ADD = mybir.AluOpType.add
+
+P = 128
+G = K // 512
+H = T // 2
+
+
+def tile_routed_moe_kernel(tc, xT, w, b, gate, offs, out):
+    nc = tc.nc
+    with ExitStack() as ctx:
+        keep = ctx.enter_context(tc.tile_pool(name="keep", bufs=1))
+        psum = ctx.enter_context(tc.psum_pool(name="psum", bufs=1))
+
+        offsets = keep.tile([P, S // 16], U16, name="offsets")
+        nc.sync.dma_start(offsets[:], offs)
+
+        b_sb = keep.tile([P, E], F32, name="b_sb")
+        nc.scalar.dma_start(b_sb[:], b)
+
+        x_view = xT.rearrange("(g p u e) n -> g u p e n", g=G, p=P, u=2, e=2)
+        x_raw = {}
+        for g in range(G):
+            for u in range(2):
+                x_raw[(g, u)] = keep.tile([P, 2, T], F32, name="x_raw%d%d" % (g, u))
+                if g == 0 and u == 0:
+                    nc.sync.dma_start(x_raw[(g, u)][:, :, 0:H], x_view[g, u][:, :, 0:H])
+                    nc.sync.dma_start(x_raw[(g, u)][:, :, H:T], x_view[g, u][:, :, H:T])
+                else:
+                    nc.sync.dma_start(x_raw[(g, u)][:], x_view[g, u])
+
+        w_raw = []
+        gate_sb = keep.tile([P, S], F32, name="gate_sb")
+        for e in range(E):
+            w_raw.append(keep.tile([P, G, 4, N], F32, name="w_raw%d" % e))
+            nc.sync.dma_start(w_raw[e][:], w[e].rearrange("(g p j) n -> p g j n", g=G, p=P, j=4))
+            if e == 1:
+                nc.sync.dma_start(gate_sb[:], gate)
+
+        warm_in = keep.tile([P, 1], F32, name="warm_in")
+        warm_out = keep.tile([P, 1], F32, name="warm_out")
+        nc.gpsimd.memset(warm_in[:], 0.0)
+        nc.scalar.activation(out=warm_out[:], in_=warm_in[:], func=GELU)
+
+        pairs = keep.tile([P, 5 * T, 2], BF16, name="pairs")
+        nc.gpsimd.memset(pairs[:, 4 * T : 5 * T, :], 0.0)
+        pair_words = pairs[:].rearrange("p n e -> p (n e)").bitcast(U32)
+
+        def gp_cast(dst, src):
+            nc.gpsimd.tensor_scalar(out=dst, in0=src, scalar1=1.0, scalar2=0.0, op0=MULT, op1=ADD)
+
+        xc = keep.tile([P, G * S], U32, name="xc", align_bytes=64)
+        xs = keep.tile([P, G * S], U8, name="xs", align_bytes=64)
+        xi = keep.tile([P, G, S, 4], BF16, name="xi", align_bytes=64)
+        xi_words = xi[:].rearrange("p g s t -> p (g s t)").bitcast(U32).rearrange("p (g s u) -> p g s u", g=G, u=2)
+
+        def gather_x(g, u):
+            blk = 3 - (2 * g + u)
+            dst = pairs[:, blk * T : (blk + 1) * T, :]
+            src = x_raw[(g, u)][:].rearrange("p e n -> p n e")
+            nc.scalar.copy(out=dst[:, 0:H, :], in_=src[:, 0:H, :])
+            if g == 0 and u == 0:
+                nc.vector.tensor_copy(out=dst[:, H:T, :], in_=src[:, H:T, :])
+            else:
+                gp_cast(dst[:, H:T, :], src[:, H:T, :])
+            nc.vector.tensor_copy(
+                out=xi_words[:, g, :, u],
+                in_=pair_words[:, blk * T : (blk + 2) * T].indirect(offsets[:]),
+            )
+
+        def quantize_x(g):
+            nc.vector.quantize_mx(
+                out=xc[:, g * S : (g + 1) * S].bitcast(FP8X4),
+                scales=xs[:, g * S : (g + 1) * S],
+                in_=xi[:, g].rearrange("p s t -> p (s t)"),
+            )
+
+        wc = keep.tile([P, E, G * N], U32, name="wc", align_bytes=64)
+        ws = keep.tile([P, E, G * N], U8, name="ws", align_bytes=64)
+        wi = keep.tile([P, E, G, N, 4], BF16, name="wi", align_bytes=64)
+        res = keep.tile([P, T], F32, name="res")
+        y = keep.tile([P, S], F32, name="y")
+
+        def cast_w(e):
+            gp_cast(wi[:, e, 0], w_raw[e][:, 0].rearrange("p j n -> p n j"))
+            nc.scalar.copy(out=wi[:, e, 1], in_=w_raw[e][:, 1].rearrange("p j n -> p n j"))
+
+        def quantize_w(e0, e1):
+            nc.vector.quantize_mx(
+                out=wc[:, e0:e1, :].rearrange("p e c -> p (e c)").bitcast(FP8X4),
+                scales=ws[:, e0:e1, :].rearrange("p e c -> p (e c)"),
+                in_=wi[:, e0:e1].rearrange("p e g n j -> p (e g n j)"),
+            )
+
+        def multiply(e):
+            acc = psum.tile([P, C], F32, name="acc%d" % e)
+            for g in range(G):
+                nc.tensor.matmul_mx(
+                    out=acc[:],
+                    lhsT=wc[:, e, g * N : (g + 1) * N].bitcast(FP8X4),
+                    lhsT_scale=ws[:, e, g * N : (g + 1) * N],
+                    rhs=xc[:, g * S + e * C : g * S + (e + 1) * C].bitcast(FP8X4),
+                    rhs_scale=xs[:, g * S + e * C : g * S + (e + 1) * C],
+                    start=(g == 0),
+                    stop=(g == G - 1),
+                )
+            nc.scalar.activation(out=y[:, e * C : (e + 1) * C], in_=acc[:], func=GELU, bias=b_sb[:, e : e + 1])
+
+        def scatter(e0, e1):
+            nc.vector.tensor_tensor(
+                out=res[:].indirect(offsets[:, e0 * (C // 16) : e1 * (C // 16)]),
+                in0=y[:, e0 * C : e1 * C],
+                in1=gate_sb[:, e0 * C : e1 * C],
+                op=MULT,
+            )
+
+        gather_x(0, 0)
+        gather_x(0, 1)
+        gather_x(1, 0)
+        quantize_x(0)
+        gather_x(1, 1)
+        cast_w(0)
+        quantize_w(0, 1)
+        quantize_x(1)
+        for e in range(1, E):
+            cast_w(e)
+            quantize_w(e, e + 1)
+        for e in range(E):
+            multiply(e)
+        scatter(0, 1)
+        scatter(1, 2)
+        scatter(2, 4)
+        nc.sync.dma_start(out, res[:])

@@ -13,6 +13,7 @@ U16 = mybir.dt.uint16
 U8 = mybir.dt.uint8
 FP8X4 = mybir.dt.float8_e4m3fn_x4
 GELU = mybir.ActivationFunctionType.Gelu_apprx_tanh
+COPY = mybir.ActivationFunctionType.Copy
 MULT = mybir.AluOpType.mult
 ADD = mybir.AluOpType.add
 
@@ -64,10 +65,16 @@ def tile_routed_moe_kernel(tc, xT, w, b, gate, offs, out):
         def gp_cast(dst, src):
             nc.gpsimd.tensor_scalar(out=dst, in0=src, scalar1=1.0, scalar2=0.0, op0=MULT, op1=ADD)
 
+        def sc_cast(dst, src):
+            nc.scalar.copy(out=dst, in_=src)
+
         xc = keep.tile([P, G * S], U32, name="xc", align_bytes=64)
         xs = keep.tile([P, G * S], U8, name="xs", align_bytes=64)
         xi = keep.tile([P, G, S, 4], BF16, name="xi", align_bytes=64)
-        xi_words = xi[:].rearrange("p g s t -> p (g s t)").bitcast(U32).rearrange("p (g s u) -> p g s u", g=G, u=2)
+        xi_f32 = xi[:].rearrange("p g s t -> p (g s t)").bitcast(F32).rearrange("p (g s u) -> p g s u", g=G, u=2)
+        gw0 = keep.tile([P, 2, S], F32, name="gw0")
+        gw1 = keep.tile([P, 2, S], F32, name="gw1", tag="late", align_bytes=64)
+        gw = [gw0, gw1]
 
         def gather_x(g, u):
             blk = 3 - (2 * g + u)
@@ -79,9 +86,12 @@ def tile_routed_moe_kernel(tc, xT, w, b, gate, offs, out):
             else:
                 gp_cast(dst[:, H:T, :], src[:, H:T, :])
             nc.vector.tensor_copy(
-                out=xi_words[:, g, :, u],
+                out=gw[g][:, u, :].bitcast(U32),
                 in_=pair_words[:, blk * T : (blk + 2) * T].indirect(offsets[:]),
             )
+
+        def interleave(g):
+            nc.scalar.copy(out=xi_f32[:, g], in_=gw[g][:].rearrange("p u s -> p s u"))
 
         def quantize_x(g):
             nc.vector.quantize_mx(
@@ -92,19 +102,20 @@ def tile_routed_moe_kernel(tc, xT, w, b, gate, offs, out):
 
         wc = keep.tile([P, E, G * N], U32, name="wc", align_bytes=64)
         ws = keep.tile([P, E, G * N], U8, name="ws", align_bytes=64)
-        wi = keep.tile([P, E, G, N, 4], BF16, name="wi", align_bytes=64)
+        wi0 = keep.tile([P, G, N, 4], BF16, name="wi0", align_bytes=64)
+        wi = [wi0[:]]
         res = keep.tile([P, T], F32, name="res")
         y = keep.tile([P, S], F32, name="y")
 
-        def cast_w(e):
-            gp_cast(wi[:, e, 0], w_raw[e][:, 0].rearrange("p j n -> p n j"))
-            nc.scalar.copy(out=wi[:, e, 1], in_=w_raw[e][:, 1].rearrange("p j n -> p n j"))
+        def cast_w(e, first, second):
+            first(wi[e][:, 0], w_raw[e][:, 0].rearrange("p j n -> p n j"))
+            second(wi[e][:, 1], w_raw[e][:, 1].rearrange("p j n -> p n j"))
 
-        def quantize_w(e0, e1):
+        def quantize_w(e):
             nc.vector.quantize_mx(
-                out=wc[:, e0:e1, :].rearrange("p e c -> p (e c)").bitcast(FP8X4),
-                scales=ws[:, e0:e1, :].rearrange("p e c -> p (e c)"),
-                in_=wi[:, e0:e1].rearrange("p e g n j -> p (e g n j)"),
+                out=wc[:, e, :].bitcast(FP8X4),
+                scales=ws[:, e, :],
+                in_=wi[e].rearrange("p g n j -> p (g n j)"),
             )
 
         def multiply(e):
@@ -132,16 +143,25 @@ def tile_routed_moe_kernel(tc, xT, w, b, gate, offs, out):
         gather_x(0, 0)
         gather_x(0, 1)
         gather_x(1, 0)
-        quantize_x(0)
         gather_x(1, 1)
-        cast_w(0)
-        quantize_w(0, 1)
+        interleave(0)
+        interleave(1)
+        quantize_x(0)
+        cast_w(0, gp_cast, gp_cast)
+        quantize_w(0)
         quantize_x(1)
-        for e in range(1, E):
-            cast_w(e)
-            quantize_w(e, e + 1)
-        for e in range(E):
-            multiply(e)
+        wi123 = keep.tile([P, 3, G, N, 4], BF16, name="wi123", tag="late", align_bytes=64)
+        wi.extend([wi123[:, 0], wi123[:, 1], wi123[:, 2]])
+        cast_w(1, gp_cast, sc_cast)
+        quantize_w(1)
+        cast_w(2, gp_cast, sc_cast)
+        quantize_w(2)
+        multiply(0)
+        cast_w(3, gp_cast, sc_cast)
+        quantize_w(3)
+        multiply(1)
+        multiply(2)
+        multiply(3)
         scatter(0, 1)
         scatter(1, 2)
         scatter(2, 4)

@@ -68,6 +68,12 @@ def tile_routed_moe_kernel(tc, xT, w, b, gate, offs, out):
         def sc_cast(dst, src):
             nc.scalar.copy(out=dst, in_=src)
 
+        def by_fours(dst):
+            return dst.rearrange("p (c i) r -> p c r i", i=4)
+
+        def rows_by_fours(src):
+            return src.rearrange("p r (c i) -> p c r i", i=4)
+
         xc = keep.tile([P, G * S], U32, name="xc", align_bytes=64)
         xs = keep.tile([P, G * S], U8, name="xs", align_bytes=64)
         xi = keep.tile([P, G, S, 4], BF16, name="xi", align_bytes=64)
@@ -79,19 +85,19 @@ def tile_routed_moe_kernel(tc, xT, w, b, gate, offs, out):
         def gather_x(g, u):
             blk = 3 - (2 * g + u)
             dst = pairs[:, blk * T : (blk + 1) * T, :]
-            src = x_raw[(g, u)][:].rearrange("p e n -> p n e")
-            nc.scalar.copy(out=dst[:, 0:H, :], in_=src[:, 0:H, :])
+            raw = x_raw[(g, u)]
+            sc_cast(by_fours(dst[:, 0:H, :]), rows_by_fours(raw[:, :, 0:H]))
             if g == 0 and u == 0:
-                nc.vector.tensor_copy(out=dst[:, H:T, :], in_=src[:, H:T, :])
+                nc.vector.tensor_copy(out=dst[:, H:T, :], in_=raw[:, :, H:T].rearrange("p e n -> p n e"))
             else:
-                gp_cast(dst[:, H:T, :], src[:, H:T, :])
+                gp_cast(by_fours(dst[:, H:T, :]), rows_by_fours(raw[:, :, H:T]))
             nc.vector.tensor_copy(
                 out=gw[g][:, u, :].bitcast(U32),
                 in_=pair_words[:, blk * T : (blk + 2) * T].indirect(offsets[:]),
             )
 
         def interleave(g):
-            nc.scalar.copy(out=xi_f32[:, g], in_=gw[g][:].rearrange("p u s -> p s u"))
+            sc_cast(by_fours(xi_f32[:, g]), rows_by_fours(gw[g][:]))
 
         def quantize_x(g):
             nc.vector.quantize_mx(
@@ -108,8 +114,8 @@ def tile_routed_moe_kernel(tc, xT, w, b, gate, offs, out):
         y = keep.tile([P, S], F32, name="y")
 
         def cast_w(e, first, second):
-            first(wi[e][:, 0], w_raw[e][:, 0].rearrange("p j n -> p n j"))
-            second(wi[e][:, 1], w_raw[e][:, 1].rearrange("p j n -> p n j"))
+            first(by_fours(wi[e][:, 0]), rows_by_fours(w_raw[e][:, 0]))
+            second(by_fours(wi[e][:, 1]), rows_by_fours(w_raw[e][:, 1]))
 
         def quantize_w(e):
             nc.vector.quantize_mx(

@@ -117,6 +117,11 @@ def tile_routed_moe_kernel(tc, xT, w, b, gate, offs, out):
             first(by_fours(wi[e][:, 0]), rows_by_fours(w_raw[e][:, 0]))
             second(by_fours(wi[e][:, 1]), rows_by_fours(w_raw[e][:, 1]))
 
+        def cast_w_quarter(e):
+            gp_cast(by_fours(wi[e][:, 0, 0 : N // 2, :]), rows_by_fours(w_raw[e][:, 0, :, 0 : N // 2]))
+            sc_cast(by_fours(wi[e][:, 0, N // 2 : N, :]), rows_by_fours(w_raw[e][:, 0, :, N // 2 : N]))
+            sc_cast(by_fours(wi[e][:, 1]), rows_by_fours(w_raw[e][:, 1]))
+
         def quantize_w(e):
             nc.vector.quantize_mx(
                 out=wc[:, e, :].bitcast(FP8X4),
@@ -158,12 +163,12 @@ def tile_routed_moe_kernel(tc, xT, w, b, gate, offs, out):
         quantize_x(1)
         wi123 = keep.tile([P, 3, G, N, 4], BF16, name="wi123", tag="late", align_bytes=64)
         wi.extend([wi123[:, 0], wi123[:, 1], wi123[:, 2]])
-        cast_w(1, gp_cast, sc_cast)
+        cast_w_quarter(1)
         quantize_w(1)
-        cast_w(2, gp_cast, sc_cast)
+        cast_w_quarter(2)
         quantize_w(2)
         multiply(0)
-        cast_w(3, gp_cast, sc_cast)
+        cast_w_quarter(3)
         quantize_w(3)
         multiply(1)
         multiply(2)

@@ -99,6 +99,10 @@ def tile_routed_moe_kernel(tc, xT, w, b, gate, offs, out):
         def interleave(g):
             sc_cast(by_fours(xi_f32[:, g]), rows_by_fours(gw[g][:]))
 
+        def interleave_shared(g):
+            sc_cast(by_fours(xi_f32[:, g, 0:H, :]), rows_by_fours(gw[g][:, :, 0:H]))
+            nc.vector.tensor_copy(out=xi_f32[:, g, H:S, :], in_=gw[g][:, :, H:S].rearrange("p u s -> p s u"))
+
         def quantize_x(g):
             nc.vector.quantize_mx(
                 out=xc[:, g * S : (g + 1) * S].bitcast(FP8X4),
@@ -156,7 +160,7 @@ def tile_routed_moe_kernel(tc, xT, w, b, gate, offs, out):
         gather_x(1, 0)
         gather_x(1, 1)
         interleave(0)
-        interleave(1)
+        interleave_shared(1)
         quantize_x(0)
         cast_w(0, gp_cast, gp_cast)
         quantize_w(0)

@@ -29,8 +29,6 @@ def tile_routed_moe_kernel(tc, xT, w, b, gate, offs, out):
         psum = ctx.enter_context(tc.psum_pool(name="psum", bufs=1))
 
         offsets = keep.tile([P, S // 16], U16, name="offsets")
-        nc.sync.dma_start(offsets[:], offs)
-
         b_sb = keep.tile([P, E], F32, name="b_sb")
         nc.scalar.dma_start(b_sb[:], b)
 
@@ -41,6 +39,7 @@ def tile_routed_moe_kernel(tc, xT, w, b, gate, offs, out):
                 x_raw[(g, u)] = keep.tile([P, 2, T], F32, name="x_raw%d%d" % (g, u))
                 if g == 0 and u == 0:
                     nc.sync.dma_start(x_raw[(g, u)][:, :, 0:H], x_view[g, u][:, :, 0:H])
+                    nc.sync.dma_start(offsets[:], offs)
                     nc.sync.dma_start(x_raw[(g, u)][:, :, H:T], x_view[g, u][:, :, H:T])
                 else:
                     nc.sync.dma_start(x_raw[(g, u)][:], x_view[g, u])
@@ -121,10 +120,8 @@ def tile_routed_moe_kernel(tc, xT, w, b, gate, offs, out):
             first(by_fours(wi[e][:, 0]), rows_by_fours(w_raw[e][:, 0]))
             second(by_fours(wi[e][:, 1]), rows_by_fours(w_raw[e][:, 1]))
 
-        def cast_w_quarter(e):
-            gp_cast(by_fours(wi[e][:, 0, 0 : N // 2, :]), rows_by_fours(w_raw[e][:, 0, :, 0 : N // 2]))
-            sc_cast(by_fours(wi[e][:, 0, N // 2 : N, :]), rows_by_fours(w_raw[e][:, 0, :, N // 2 : N]))
-            sc_cast(by_fours(wi[e][:, 1]), rows_by_fours(w_raw[e][:, 1]))
+        def cast_w_whole(e):
+            sc_cast(wi[e].rearrange("p g (c i) j -> p g c j i", i=4), w_raw[e][:].rearrange("p g j (c i) -> p g c j i", i=4))
 
         def quantize_w(e):
             nc.vector.quantize_mx(
@@ -167,12 +164,12 @@ def tile_routed_moe_kernel(tc, xT, w, b, gate, offs, out):
         quantize_x(1)
         wi123 = keep.tile([P, 3, G, N, 4], BF16, name="wi123", tag="late", align_bytes=64)
         wi.extend([wi123[:, 0], wi123[:, 1], wi123[:, 2]])
-        cast_w_quarter(1)
+        cast_w_whole(1)
         quantize_w(1)
-        cast_w_quarter(2)
+        cast_w_whole(2)
         quantize_w(2)
         multiply(0)
-        cast_w_quarter(3)
+        cast_w_whole(3)
         quantize_w(3)
         multiply(1)
         multiply(2)

@@ -37,12 +37,9 @@ def tile_routed_moe_kernel(tc, xT, w, b, gate, offs, out):
         for g in range(G):
             for u in range(2):
                 x_raw[(g, u)] = keep.tile([P, 2, T], F32, name="x_raw%d%d" % (g, u))
+                nc.sync.dma_start(x_raw[(g, u)][:], x_view[g, u])
                 if g == 0 and u == 0:
-                    nc.sync.dma_start(x_raw[(g, u)][:, :, 0:H], x_view[g, u][:, :, 0:H])
                     nc.sync.dma_start(offsets[:], offs)
-                    nc.sync.dma_start(x_raw[(g, u)][:, :, H:T], x_view[g, u][:, :, H:T])
-                else:
-                    nc.sync.dma_start(x_raw[(g, u)][:], x_view[g, u])
 
         w_raw = []
         gate_sb = keep.tile([P, S], F32, name="gate_sb")
@@ -85,11 +82,13 @@ def tile_routed_moe_kernel(tc, xT, w, b, gate, offs, out):
             blk = 3 - (2 * g + u)
             dst = pairs[:, blk * T : (blk + 1) * T, :]
             raw = x_raw[(g, u)]
-            sc_cast(by_fours(dst[:, 0:H, :]), rows_by_fours(raw[:, :, 0:H]))
             if g == 0 and u == 0:
-                nc.vector.tensor_copy(out=dst[:, H:T, :], in_=raw[:, :, H:T].rearrange("p e n -> p n e"))
+                cut = 3 * T // 8
+                nc.vector.tensor_copy(out=dst[:, cut:T, :], in_=raw[:, :, cut:T].rearrange("p e n -> p n e"))
             else:
-                gp_cast(by_fours(dst[:, H:T, :]), rows_by_fours(raw[:, :, H:T]))
+                cut = H
+                gp_cast(by_fours(dst[:, cut:T, :]), rows_by_fours(raw[:, :, cut:T]))
+            sc_cast(by_fours(dst[:, 0:cut, :]), rows_by_fours(raw[:, :, 0:cut]))
             nc.vector.tensor_copy(
                 out=gw[g][:, u, :].bitcast(U32),
                 in_=pair_words[:, blk * T : (blk + 2) * T].indirect(offsets[:]),
@@ -160,8 +159,8 @@ def tile_routed_moe_kernel(tc, xT, w, b, gate, offs, out):
         interleave_shared(1)
         quantize_x(0)
         cast_w(0, gp_cast, gp_cast)
-        quantize_w(0)
         quantize_x(1)
+        quantize_w(0)
         wi123 = keep.tile([P, 3, G, N, 4], BF16, name="wi123", tag="late", align_bytes=64)
         wi.extend([wi123[:, 0], wi123[:, 1], wi123[:, 2]])
         cast_w_whole(1)

@@ -45,7 +45,12 @@ def tile_routed_moe_kernel(tc, xT, w, b, gate, offs, out):
         gate_sb = keep.tile([P, S], F32, name="gate_sb")
         for e in range(E):
             w_raw.append(keep.tile([P, G, 4, N], F32, name="w_raw%d" % e))
-            nc.sync.dma_start(w_raw[e][:], w[e].rearrange("(g p j) n -> p g j n", g=G, p=P, j=4))
+            w_view = w[e].rearrange("(g p j) n -> p g j n", g=G, p=P, j=4)
+            if e < E - 1:
+                nc.sync.dma_start(w_raw[e][:], w_view)
+            else:
+                nc.sync.dma_start(w_raw[e][:, 0], w_view[:, 0])
+                nc.sync.dma_start(w_raw[e][:, 1], w_view[:, 1])
             if e == 1:
                 nc.sync.dma_start(gate_sb[:], gate)
 
@@ -122,6 +127,11 @@ def tile_routed_moe_kernel(tc, xT, w, b, gate, offs, out):
         def cast_w_whole(e):
             sc_cast(wi[e].rearrange("p g (c i) j -> p g c j i", i=4), w_raw[e][:].rearrange("p g j (c i) -> p g c j i", i=4))
 
+        def cast_w_last(e):
+            sc_cast(by_fours(wi[e][:, 0]), rows_by_fours(w_raw[e][:, 0]))
+            sc_cast(by_fours(wi[e][:, 1, 0 : N // 2, :]), rows_by_fours(w_raw[e][:, 1, :, 0 : N // 2]))
+            gp_cast(by_fours(wi[e][:, 1, N // 2 : N, :]), rows_by_fours(w_raw[e][:, 1, :, N // 2 : N]))
+
         def quantize_w(e):
             nc.vector.quantize_mx(
                 out=wc[:, e, :].bitcast(FP8X4),
@@ -168,7 +178,7 @@ def tile_routed_moe_kernel(tc, xT, w, b, gate, offs, out):
         cast_w_whole(2)
         quantize_w(2)
         multiply(0)
-        cast_w_whole(3)
+        cast_w_last(3)
         quantize_w(3)
         multiply(1)
         multiply(2)

@@ -51,7 +51,7 @@ def tile_routed_moe_kernel(tc, xT, w, b, gate, offs, out):
             else:
                 nc.sync.dma_start(w_raw[e][:, 0], w_view[:, 0])
                 nc.sync.dma_start(w_raw[e][:, 1], w_view[:, 1])
-            if e == 1:
+            if e == 2:
                 nc.sync.dma_start(gate_sb[:], gate)
 
         warm_in = keep.tile([P, 1], F32, name="warm_in")
@@ -79,7 +79,7 @@ def tile_routed_moe_kernel(tc, xT, w, b, gate, offs, out):
         xs = keep.tile([P, G * S], U8, name="xs", align_bytes=64)
         xi = keep.tile([P, G, S, 4], BF16, name="xi", align_bytes=64)
         xi_f32 = xi[:].rearrange("p g s t -> p (g s t)").bitcast(F32).rearrange("p (g s u) -> p g s u", g=G, u=2)
-        gw0 = keep.tile([P, 2, S], F32, name="gw0")
+        gw0 = keep.tile([P, 2, S], F32, name="gw0", tag="early", align_bytes=64)
         gw1 = keep.tile([P, 2, S], F32, name="gw1", tag="late", align_bytes=64)
         gw = [gw0, gw1]
 
@@ -99,12 +99,11 @@ def tile_routed_moe_kernel(tc, xT, w, b, gate, offs, out):
                 in_=pair_words[:, blk * T : (blk + 2) * T].indirect(offsets[:]),
             )
 
-        def interleave(g):
+        def interleave_by_scalar(g):
             sc_cast(by_fours(xi_f32[:, g]), rows_by_fours(gw[g][:]))
 
-        def interleave_shared(g):
-            sc_cast(by_fours(xi_f32[:, g, 0:H, :]), rows_by_fours(gw[g][:, :, 0:H]))
-            nc.vector.tensor_copy(out=xi_f32[:, g, H:S, :], in_=gw[g][:, :, H:S].rearrange("p u s -> p s u"))
+        def interleave_by_vector(g):
+            nc.vector.tensor_copy(out=xi_f32[:, g], in_=gw[g][:].rearrange("p u s -> p s u"))
 
         def quantize_x(g):
             nc.vector.quantize_mx(
@@ -113,7 +112,9 @@ def tile_routed_moe_kernel(tc, xT, w, b, gate, offs, out):
                 in_=xi[:, g].rearrange("p s t -> p (s t)"),
             )
 
-        wc = keep.tile([P, E, G * N], U32, name="wc", align_bytes=64)
+        wc0 = keep.tile([P, G * N], U32, name="wc0", tag="codes0", align_bytes=64)
+        wc123 = keep.tile([P, E - 1, G * N], U32, name="wc123", align_bytes=64)
+        wc = [wc0[:], wc123[:, 0], wc123[:, 1], wc123[:, 2]]
         ws = keep.tile([P, E, G * N], U8, name="ws", align_bytes=64)
         wi0 = keep.tile([P, G, N, 4], BF16, name="wi0", align_bytes=64)
         wi = [wi0[:]]
@@ -134,7 +135,7 @@ def tile_routed_moe_kernel(tc, xT, w, b, gate, offs, out):
 
         def quantize_w(e):
             nc.vector.quantize_mx(
-                out=wc[:, e, :].bitcast(FP8X4),
+                out=wc[e].bitcast(FP8X4),
                 scales=ws[:, e, :],
                 in_=wi[e].rearrange("p g n j -> p (g n j)"),
             )
@@ -144,7 +145,7 @@ def tile_routed_moe_kernel(tc, xT, w, b, gate, offs, out):
             for g in range(G):
                 nc.tensor.matmul_mx(
                     out=acc[:],
-                    lhsT=wc[:, e, g * N : (g + 1) * N].bitcast(FP8X4),
+                    lhsT=wc[e][:, g * N : (g + 1) * N].bitcast(FP8X4),
                     lhsT_scale=ws[:, e, g * N : (g + 1) * N],
                     rhs=xc[:, g * S + e * C : g * S + (e + 1) * C].bitcast(FP8X4),
                     rhs_scale=xs[:, g * S + e * C : g * S + (e + 1) * C],
@@ -165,19 +166,22 @@ def tile_routed_moe_kernel(tc, xT, w, b, gate, offs, out):
         gather_x(0, 1)
         gather_x(1, 0)
         gather_x(1, 1)
-        interleave(0)
-        interleave_shared(1)
+        interleave_by_scalar(0)
+        interleave_by_vector(1)
         quantize_x(0)
         cast_w(0, gp_cast, gp_cast)
         quantize_x(1)
         quantize_w(0)
-        wi123 = keep.tile([P, 3, G, N, 4], BF16, name="wi123", tag="late", align_bytes=64)
-        wi.extend([wi123[:, 0], wi123[:, 1], wi123[:, 2]])
+        wi1 = keep.tile([P, G, N, 4], BF16, name="wi1", tag="early", align_bytes=64)
+        wi2 = keep.tile([P, G, N, 4], BF16, name="wi2", tag="late", align_bytes=64)
+        wi.extend([wi1[:], wi2[:]])
         cast_w_whole(1)
         quantize_w(1)
         cast_w_whole(2)
         quantize_w(2)
         multiply(0)
+        wi3 = keep.tile([P, G, N, 4], BF16, name="wi3", tag="codes0", align_bytes=64)
+        wi.append(wi3[:])
         cast_w_last(3)
         quantize_w(3)
         multiply(1)

@@ -116,22 +116,16 @@ def tile_routed_moe_kernel(tc, xT, w, b, gate, offs, out):
         wc123 = keep.tile([P, E - 1, G * N], U32, name="wc123", align_bytes=64)
         wc = [wc0[:], wc123[:, 0], wc123[:, 1], wc123[:, 2]]
         ws = keep.tile([P, E, G * N], U8, name="ws", align_bytes=64)
-        wi0 = keep.tile([P, G, N, 4], BF16, name="wi0", align_bytes=64)
-        wi = [wi0[:]]
+        wi = []
         res = keep.tile([P, T], F32, name="res")
         y = keep.tile([P, S], F32, name="y")
-
-        def cast_w(e, first, second):
-            first(by_fours(wi[e][:, 0]), rows_by_fours(w_raw[e][:, 0]))
-            second(by_fours(wi[e][:, 1]), rows_by_fours(w_raw[e][:, 1]))
 
         def cast_w_whole(e):
             sc_cast(wi[e].rearrange("p g (c i) j -> p g c j i", i=4), w_raw[e][:].rearrange("p g j (c i) -> p g c j i", i=4))
 
         def cast_w_last(e):
-            sc_cast(by_fours(wi[e][:, 0]), rows_by_fours(w_raw[e][:, 0]))
-            sc_cast(by_fours(wi[e][:, 1, 0 : N // 2, :]), rows_by_fours(w_raw[e][:, 1, :, 0 : N // 2]))
-            gp_cast(by_fours(wi[e][:, 1, N // 2 : N, :]), rows_by_fours(w_raw[e][:, 1, :, N // 2 : N]))
+            for g in range(G):
+                sc_cast(by_fours(wi[e][:, g]), rows_by_fours(w_raw[e][:, g]))
 
         def quantize_w(e):
             nc.vector.quantize_mx(
@@ -169,12 +163,13 @@ def tile_routed_moe_kernel(tc, xT, w, b, gate, offs, out):
         interleave_by_scalar(0)
         interleave_by_vector(1)
         quantize_x(0)
-        cast_w(0, gp_cast, gp_cast)
+        wi01 = keep.tile([P, 2, G, N, 4], BF16, name="wi01", tag="early", align_bytes=64)
+        wi.extend([wi01[:, 0], wi01[:, 1]])
+        cast_w_whole(0)
         quantize_x(1)
         quantize_w(0)
-        wi1 = keep.tile([P, G, N, 4], BF16, name="wi1", tag="early", align_bytes=64)
         wi2 = keep.tile([P, G, N, 4], BF16, name="wi2", tag="late", align_bytes=64)
-        wi.extend([wi1[:], wi2[:]])
+        wi.append(wi2[:])
         cast_w_whole(1)
         quantize_w(1)
         cast_w_whole(2)

@@ -75,7 +75,8 @@ def tile_routed_moe_kernel(tc, xT, w, b, gate, offs, out):
         def rows_by_fours(src):
             return src.rearrange("p r (c i) -> p c r i", i=4)
 
-        xc = keep.tile([P, G * S], U32, name="xc", align_bytes=64)
+        xc0 = keep.tile([P, S], U32, name="xc0", align_bytes=64)
+        xc1a = keep.tile([P, H], U32, name="xc1a", align_bytes=64)
         xs = keep.tile([P, G * S], U8, name="xs", align_bytes=64)
         xi = keep.tile([P, G, S, 4], BF16, name="xi", align_bytes=64)
         xi_f32 = xi[:].rearrange("p g s t -> p (g s t)").bitcast(F32).rearrange("p (g s u) -> p g s u", g=G, u=2)
@@ -105,11 +106,11 @@ def tile_routed_moe_kernel(tc, xT, w, b, gate, offs, out):
         def interleave_by_vector(g):
             nc.vector.tensor_copy(out=xi_f32[:, g], in_=gw[g][:].rearrange("p u s -> p s u"))
 
-        def quantize_x(g):
+        def quantize_x(g, s0, s1, codes):
             nc.vector.quantize_mx(
-                out=xc[:, g * S : (g + 1) * S].bitcast(FP8X4),
-                scales=xs[:, g * S : (g + 1) * S],
-                in_=xi[:, g].rearrange("p s t -> p (s t)"),
+                out=codes[:].bitcast(FP8X4),
+                scales=xs[:, g * S + s0 : g * S + s1],
+                in_=xi[:, g, s0:s1].rearrange("p s t -> p (s t)"),
             )
 
         wc0 = keep.tile([P, G * N], U32, name="wc0", tag="codes0", align_bytes=64)
@@ -134,6 +135,13 @@ def tile_routed_moe_kernel(tc, xT, w, b, gate, offs, out):
                 in_=wi[e].rearrange("p g n j -> p (g n j)"),
             )
 
+        def token_codes(g, e):
+            if g == 0:
+                return xc0[:, e * C : (e + 1) * C]
+            if e < 2:
+                return xc1a[:, e * C : (e + 1) * C]
+            return xc1b[:, (e - 2) * C : (e - 1) * C]
+
         def multiply(e):
             acc = psum.tile([P, C], F32, name="acc%d" % e)
             for g in range(G):
@@ -141,7 +149,7 @@ def tile_routed_moe_kernel(tc, xT, w, b, gate, offs, out):
                     out=acc[:],
                     lhsT=wc[e][:, g * N : (g + 1) * N].bitcast(FP8X4),
                     lhsT_scale=ws[:, e, g * N : (g + 1) * N],
-                    rhs=xc[:, g * S + e * C : g * S + (e + 1) * C].bitcast(FP8X4),
+                    rhs=token_codes(g, e).bitcast(FP8X4),
                     rhs_scale=xs[:, g * S + e * C : g * S + (e + 1) * C],
                     start=(g == 0),
                     stop=(g == G - 1),
@@ -162,16 +170,18 @@ def tile_routed_moe_kernel(tc, xT, w, b, gate, offs, out):
         gather_x(1, 1)
         interleave_by_scalar(0)
         interleave_by_vector(1)
-        quantize_x(0)
+        quantize_x(0, 0, S, xc0)
         wi01 = keep.tile([P, 2, G, N, 4], BF16, name="wi01", tag="early", align_bytes=64)
         wi.extend([wi01[:, 0], wi01[:, 1]])
         cast_w_whole(0)
-        quantize_x(1)
+        quantize_x(1, 0, H, xc1a)
         quantize_w(0)
         wi2 = keep.tile([P, G, N, 4], BF16, name="wi2", tag="late", align_bytes=64)
         wi.append(wi2[:])
         cast_w_whole(1)
         quantize_w(1)
+        xc1b = keep.tile([P, H], U32, name="xc1b", tag="early", align_bytes=64)
+        quantize_x(1, H, S, xc1b)
         cast_w_whole(2)
         quantize_w(2)
         multiply(0)

@@ -78,8 +78,8 @@ def tile_routed_moe_kernel(tc, xT, w, b, gate, offs, out):
         xc0 = keep.tile([P, S], U32, name="xc0", align_bytes=64)
         xc1a = keep.tile([P, H], U32, name="xc1a", align_bytes=64)
         xs = keep.tile([P, G * S], U8, name="xs", align_bytes=64)
-        xi = keep.tile([P, G, S, 4], BF16, name="xi", align_bytes=64)
-        xi_f32 = xi[:].rearrange("p g s t -> p (g s t)").bitcast(F32).rearrange("p (g s u) -> p g s u", g=G, u=2)
+        xi = keep.tile([P, S, 4], BF16, name="xi", align_bytes=64)
+        xi_f32 = xi[:].rearrange("p s t -> p (s t)").bitcast(F32).rearrange("p (s u) -> p s u", u=2)
         gw0 = keep.tile([P, 2, S], F32, name="gw0", tag="early", align_bytes=64)
         gw1 = keep.tile([P, 2, S], F32, name="gw1", tag="late", align_bytes=64)
         gw = [gw0, gw1]
@@ -101,16 +101,16 @@ def tile_routed_moe_kernel(tc, xT, w, b, gate, offs, out):
             )
 
         def interleave_by_scalar(g):
-            sc_cast(by_fours(xi_f32[:, g]), rows_by_fours(gw[g][:]))
+            sc_cast(by_fours(xi_f32), rows_by_fours(gw[g][:]))
 
         def interleave_by_vector(g):
-            nc.vector.tensor_copy(out=xi_f32[:, g], in_=gw[g][:].rearrange("p u s -> p s u"))
+            nc.vector.tensor_copy(out=xi_f32, in_=gw[g][:].rearrange("p u s -> p s u"))
 
         def quantize_x(g, s0, s1, codes):
             nc.vector.quantize_mx(
                 out=codes[:].bitcast(FP8X4),
                 scales=xs[:, g * S + s0 : g * S + s1],
-                in_=xi[:, g, s0:s1].rearrange("p s t -> p (s t)"),
+                in_=xi[:, s0:s1].rearrange("p s t -> p (s t)"),
             )
 
         wc0 = keep.tile([P, G * N], U32, name="wc0", tag="codes0", align_bytes=64)
@@ -169,13 +169,13 @@ def tile_routed_moe_kernel(tc, xT, w, b, gate, offs, out):
         gather_x(1, 0)
         gather_x(1, 1)
         interleave_by_scalar(0)
-        interleave_by_vector(1)
         quantize_x(0, 0, S, xc0)
+        interleave_by_vector(1)
         wi01 = keep.tile([P, 2, G, N, 4], BF16, name="wi01", tag="early", align_bytes=64)
         wi.extend([wi01[:, 0], wi01[:, 1]])
         cast_w_whole(0)
-        quantize_x(1, 0, H, xc1a)
         quantize_w(0)
+        quantize_x(1, 0, H, xc1a)
         wi2 = keep.tile([P, G, N, 4], BF16, name="wi2", tag="late", align_bytes=64)
         wi.append(wi2[:])
         cast_w_whole(1)

from contextlib import ExitStack

import concourse.mybir as mybir

K, T, E, C, N = 1024, 512, 4, 128, 128
S = E * C
FLOPS = 2 * K * N * S

F32 = mybir.dt.float32
BF16 = mybir.dt.bfloat16
U32 = mybir.dt.uint32
U16 = mybir.dt.uint16
U8 = mybir.dt.uint8
FP8X4 = mybir.dt.float8_e4m3fn_x4
GELU = mybir.ActivationFunctionType.Gelu_apprx_tanh
COPY = mybir.ActivationFunctionType.Copy
MULT = mybir.AluOpType.mult
ADD = mybir.AluOpType.add

P = 128
G = K // 512
H = T // 2


def tile_routed_moe_kernel(tc, xT, w, b, gate, offs, out):
    nc = tc.nc
    with ExitStack() as ctx:
        keep = ctx.enter_context(tc.tile_pool(name="keep", bufs=1))
        psum = ctx.enter_context(tc.psum_pool(name="psum", bufs=1))

        offsets = keep.tile([P, S // 16], U16, name="offsets")
        b_sb = keep.tile([P, E], F32, name="b_sb")
        nc.scalar.dma_start(b_sb[:], b)

        x_view = xT.rearrange("(g p u e) n -> g u p e n", g=G, p=P, u=2, e=2)
        x_raw = {}
        for g in range(G):
            for u in range(2):
                x_raw[(g, u)] = keep.tile([P, 2, T], F32, name="x_raw%d%d" % (g, u))
                nc.sync.dma_start(x_raw[(g, u)][:], x_view[g, u])
                if g == 0 and u == 0:
                    nc.sync.dma_start(offsets[:], offs)

        w_raw = []
        gate_sb = keep.tile([P, S], F32, name="gate_sb")
        for e in range(E):
            w_raw.append(keep.tile([P, G, 4, N], F32, name="w_raw%d" % e))
            w_view = w[e].rearrange("(g p j) n -> p g j n", g=G, p=P, j=4)
            if e < E - 1:
                nc.sync.dma_start(w_raw[e][:], w_view)
            else:
                nc.sync.dma_start(w_raw[e][:, 0], w_view[:, 0])
                nc.sync.dma_start(w_raw[e][:, 1], w_view[:, 1])
            if e == 2:
                nc.sync.dma_start(gate_sb[:], gate)

        warm_in = keep.tile([P, 1], F32, name="warm_in")
        warm_out = keep.tile([P, 1], F32, name="warm_out")
        nc.gpsimd.memset(warm_in[:], 0.0)
        nc.scalar.activation(out=warm_out[:], in_=warm_in[:], func=GELU)

        pairs = keep.tile([P, 5 * T, 2], BF16, name="pairs")
        nc.gpsimd.memset(pairs[:, 4 * T : 5 * T, :], 0.0)
        pair_words = pairs[:].rearrange("p n e -> p (n e)").bitcast(U32)

        def gp_cast(dst, src):
            nc.gpsimd.tensor_scalar(out=dst, in0=src, scalar1=1.0, scalar2=0.0, op0=MULT, op1=ADD)

        def sc_cast(dst, src):
            nc.scalar.copy(out=dst, in_=src)

        def by_fours(dst):
            return dst.rearrange("p (c i) r -> p c r i", i=4)

        def rows_by_fours(src):
            return src.rearrange("p r (c i) -> p c r i", i=4)

        xc0 = keep.tile([P, S], U32, name="xc0", align_bytes=64)
        xc1a = keep.tile([P, H], U32, name="xc1a", align_bytes=64)
        xs = keep.tile([P, G * S], U8, name="xs", align_bytes=64)
        xi = keep.tile([P, S, 4], BF16, name="xi", align_bytes=64)
        xi_f32 = xi[:].rearrange("p s t -> p (s t)").bitcast(F32).rearrange("p (s u) -> p s u", u=2)
        gw0 = keep.tile([P, 2, S], F32, name="gw0", tag="early", align_bytes=64)
        gw1 = keep.tile([P, 2, S], F32, name="gw1", tag="late", align_bytes=64)
        gw = [gw0, gw1]

        def gather_x(g, u):
            blk = 3 - (2 * g + u)
            dst = pairs[:, blk * T : (blk + 1) * T, :]
            raw = x_raw[(g, u)]
            if g == 0 and u == 0:
                cut = 3 * T // 8
                nc.vector.tensor_copy(out=dst[:, cut:T, :], in_=raw[:, :, cut:T].rearrange("p e n -> p n e"))
            else:
                cut = H
                gp_cast(by_fours(dst[:, cut:T, :]), rows_by_fours(raw[:, :, cut:T]))
            sc_cast(by_fours(dst[:, 0:cut, :]), rows_by_fours(raw[:, :, 0:cut]))
            nc.vector.tensor_copy(
                out=gw[g][:, u, :].bitcast(U32),
                in_=pair_words[:, blk * T : (blk + 2) * T].indirect(offsets[:]),
            )

        def interleave_by_scalar(g):
            sc_cast(by_fours(xi_f32), rows_by_fours(gw[g][:]))

        def interleave_by_vector(g):
            nc.vector.tensor_copy(out=xi_f32, in_=gw[g][:].rearrange("p u s -> p s u"))

        def quantize_x(g, s0, s1, codes):
            nc.vector.quantize_mx(
                out=codes[:].bitcast(FP8X4),
                scales=xs[:, g * S + s0 : g * S + s1],
                in_=xi[:, s0:s1].rearrange("p s t -> p (s t)"),
            )

        wc0 = keep.tile([P, G * N], U32, name="wc0", tag="codes0", align_bytes=64)
        wc123 = keep.tile([P, E - 1, G * N], U32, name="wc123", align_bytes=64)
        wc = [wc0[:], wc123[:, 0], wc123[:, 1], wc123[:, 2]]
        ws = keep.tile([P, E, G * N], U8, name="ws", align_bytes=64)
        wi = []
        res = keep.tile([P, T], F32, name="res")
        y = keep.tile([P, S], F32, name="y")

        def cast_w_whole(e):
            sc_cast(wi[e].rearrange("p g (c i) j -> p g c j i", i=4), w_raw[e][:].rearrange("p g j (c i) -> p g c j i", i=4))

        def cast_w_last(e):
            for g in range(G):
                sc_cast(by_fours(wi[e][:, g]), rows_by_fours(w_raw[e][:, g]))

        def quantize_w(e):
            nc.vector.quantize_mx(
                out=wc[e].bitcast(FP8X4),
                scales=ws[:, e, :],
                in_=wi[e].rearrange("p g n j -> p (g n j)"),
            )

        def token_codes(g, e):
            if g == 0:
                return xc0[:, e * C : (e + 1) * C]
            if e < 2:
                return xc1a[:, e * C : (e + 1) * C]
            return xc1b[:, (e - 2) * C : (e - 1) * C]

        def multiply(e):
            acc = psum.tile([P, C], F32, name="acc%d" % e)
            for g in range(G):
                nc.tensor.matmul_mx(
                    out=acc[:],
                    lhsT=wc[e][:, g * N : (g + 1) * N].bitcast(FP8X4),
                    lhsT_scale=ws[:, e, g * N : (g + 1) * N],
                    rhs=token_codes(g, e).bitcast(FP8X4),
                    rhs_scale=xs[:, g * S + e * C : g * S + (e + 1) * C],
                    start=(g == 0),
                    stop=(g == G - 1),
                )
            nc.scalar.activation(out=y[:, e * C : (e + 1) * C], in_=acc[:], func=GELU, bias=b_sb[:, e : e + 1])

        def scatter(e0, e1):
            nc.vector.tensor_tensor(
                out=res[:].indirect(offsets[:, e0 * (C // 16) : e1 * (C // 16)]),
                in0=y[:, e0 * C : e1 * C],
                in1=gate_sb[:, e0 * C : e1 * C],
                op=MULT,
            )

        gather_x(0, 0)
        gather_x(0, 1)
        gather_x(1, 0)
        gather_x(1, 1)
        interleave_by_scalar(0)
        quantize_x(0, 0, S, xc0)
        interleave_by_vector(1)
        wi01 = keep.tile([P, 2, G, N, 4], BF16, name="wi01", tag="early", align_bytes=64)
        wi.extend([wi01[:, 0], wi01[:, 1]])
        cast_w_whole(0)
        quantize_w(0)
        quantize_x(1, 0, H, xc1a)
        wi2 = keep.tile([P, G, N, 4], BF16, name="wi2", tag="late", align_bytes=64)
        wi.append(wi2[:])
        cast_w_whole(1)
        quantize_w(1)
        xc1b = keep.tile([P, H], U32, name="xc1b", tag="early", align_bytes=64)
        quantize_x(1, H, S, xc1b)
        cast_w_whole(2)
        quantize_w(2)
        multiply(0)
        wi3 = keep.tile([P, G, N, 4], BF16, name="wi3", tag="codes0", align_bytes=64)
        wi.append(wi3[:])
        cast_w_last(3)
        quantize_w(3)
        multiply(1)
        multiply(2)
        multiply(3)
        scatter(0, 1)
        scatter(1, 2)
        scatter(2, 4)
        nc.sync.dma_start(out, res[:])
